import numpy as np
import ml_dtypes


def mxq(x, axis, fmt="e4m3"):
    dtype, down = {"e4m3": (ml_dtypes.float8_e4m3fn, 7), "e5m2": (ml_dtypes.float8_e5m2, 14)}[fmt]
    v = np.moveaxis(np.asarray(x, np.float32).astype(ml_dtypes.bfloat16).astype(np.float64), axis, -1)
    blocks = v.reshape(v.shape[:-1] + (-1, 32))
    amax = np.abs(blocks).max(-1, keepdims=True)
    byte = np.maximum(np.where(amax > 0, np.frexp(amax)[1] - 1 + 127, 0) - down, 1)
    scale = np.exp2(byte - 127.0)
    codes = (blocks / scale).astype(np.float32).astype(dtype).astype(np.float64)
    return np.moveaxis((codes * scale).reshape(v.shape), -1, axis)


WIDE = False


def mx_kscale(k):
    if not WIDE:
        return np.ones(k)
    levels = np.array([10, -10, 5, -5, 0])
    if k % 512:
        return np.exp2(np.random.permutation(np.resize(levels, k // 32))).repeat(32)
    a = np.empty((k // 512, 16))
    for p in range(k // 512):
        a[p, :8] = np.random.permutation(np.resize(levels, 8))
        for g in range(8):
            far = levels[np.abs(levels - a[p, g]) >= 10]
            a[p, g + 8] = far[np.random.randint(len(far))]
    return np.exp2(a.ravel()).repeat(32)


def f64(x):
    return np.asarray(x).astype(np.float64)


def striped8(idx):
    return np.asarray(idx).reshape(8, -1, 16).transpose(0, 2, 1).reshape(128, -1).astype(np.uint16)


def unstriped8(offs):
    return offs.reshape(8, 16, -1).transpose(0, 2, 1).reshape(8, -1).astype(np.int64)


def pick8(x, idx, run):
    r = np.arange(len(x))
    return x[r[:, None], idx[r % (8 * run) // run]]


E2M1 = np.array([0.0, 0.5, 1.0, 1.5, 2.0, 3.0, 4.0, 6.0, -0.0, -0.5, -1.0, -1.5, -2.0, -3.0, -4.0, -6.0])


def pack_weight(w, fmt):
    k, n = w.shape
    w = f64(np.asarray(w, np.float32).astype(ml_dtypes.bfloat16)).reshape(k // 32, 32, n)
    amax = np.abs(w).max(1)
    if fmt == "e4m3":
        byte = np.frexp(amax)[1] - 1 + 127 - 7
    else:
        mant, ex = np.frexp(amax / 6.0)
        byte = np.where(mant > 0.5, ex, ex - 1) + 127
    byte = np.clip(np.where(amax > 0, byte, 1), 1, 254)
    scaled = (w * np.exp2(127.0 - byte)[:, None, :]).reshape(k, n).astype(np.float32)
    by_word = np.ascontiguousarray(scaled.reshape(k // 512, 128, 4, n).transpose(0, 1, 3, 2))
    if fmt == "e4m3":
        words = by_word.astype(ml_dtypes.float8_e4m3fn).view(np.uint8)
    else:
        c = by_word.astype(ml_dtypes.float4_e2m1fn).view(np.uint8) & 0xF
        words = (c[..., 0::2] | (c[..., 1::2] << 4)).reshape(k // 512, 128, 2 * n)
    return np.ascontiguousarray(words), np.ascontiguousarray(byte.astype(np.uint8).reshape(k // 512, 16, n))


def unpack_weight(words, scales, fmt):
    g, _, n = scales.shape
    words = np.ascontiguousarray(words).reshape(g, 128, n, -1)
    if fmt == "e4m3":
        vals = words.view(ml_dtypes.float8_e4m3fn).astype(np.float64)
    else:
        nib = np.empty((g, 128, n, 4), np.uint8)
        nib[..., 0::2] = words & 0xF
        nib[..., 1::2] = words >> 4
        vals = E2M1[nib]
    vals = vals * np.repeat(np.exp2(scales.astype(np.float64) - 127.0), 8, axis=1)[..., None]
    return vals.transpose(0, 1, 3, 2).reshape(g * 512, n)


D, T, U, Z, I, Q = 512, 1024, 1024, 1024, 512, 128


def setup_inputs():
    n = np.random.standard_normal
    idx = np.stack([np.random.permutation(T)[:I] for _ in range(8)])
    idx2 = np.stack([np.random.permutation(U)[:I] for _ in range(8)])
    idx3 = np.stack([np.random.permutation(Z)[:I] for _ in range(8)])
    idx4 = np.stack([np.random.permutation(Z)[:I] for _ in range(8)])
    idx5 = np.stack([np.random.permutation(Z)[:I] for _ in range(8)])
    fd = mx_kscale(D)
    keysp = pack_weight(n((D, T)) / fd[:, None], "e4m3")
    notesp = pack_weight(n((D, U)) / fd[:, None], "e2m1")
    return {
        "query": (n((D, Q)) * 1.0 / np.sqrt(D) * fd[:, None]).astype(np.float32),
        "keys_words": keysp[0],
        "keys_scales": keysp[1],
        "notes_words": notesp[0],
        "notes_scales": notesp[1],
        "lam": (np.random.uniform(0.5, 1.5, (Q, 1))).astype(np.float32),
        "offs": striped8(idx),
        "offs2": striped8(idx2),
        "offs3": striped8(idx3),
        "offs4": striped8(idx4),
        "offs5": striped8(idx5),
    }


def reference(query, keys_words, keys_scales, notes_words, notes_scales, lam, offs, offs2, offs3, offs4, offs5):
    idx = unstriped8(offs)
    idx2 = unstriped8(offs2)
    idx3 = unstriped8(offs3)
    idx4 = unstriped8(offs4)
    idx5 = unstriped8(offs5)
    keysu = unpack_weight(keys_words, keys_scales, "e4m3")
    notesu = unpack_weight(notes_words, notes_scales, "e2m1")
    queryq = mxq(f64(query), 0, "e4m3")
    a = queryq.T @ keysu
    b = queryq.T @ notesu
    f1 = np.zeros((Q, Z))
    f1[np.arange(Q)[:, None], idx3[np.arange(Q) % 128 // 16]] = pick8(a, idx, 16)
    f2 = np.zeros((Q, Z))
    f2[np.arange(Q)[:, None], idx4[np.arange(Q) % 128 // 16]] = pick8(b, idx2, 16)
    cc = f1 + f2 * f64(lam)
    y = pick8(cc, idx5, 16) + pick8(a, idx, 16)
    return y

@@ -1,0 +1,114 @@
+from contextlib import ExitStack
+
+import concourse.mybir as mybir
+
+F32 = mybir.dt.float32
+BF16 = mybir.dt.bfloat16
+I32 = mybir.dt.int32
+U32 = mybir.dt.uint32
+U16 = mybir.dt.uint16
+U8 = mybir.dt.uint8
+FP8X4 = mybir.dt.float8_e4m3fn_x4
+FP4X4 = mybir.dt.float4_e2m1fn_x4
+MULT = mybir.AluOpType.mult
+ADD = mybir.AluOpType.add
+COPY = mybir.ActivationFunctionType.Copy
+
+P = 128
+PACK = 4
+D, T, U, Z, I, Q = 512, 1024, 1024, 1024, 512, 128
+FLOPS = 2 * D * Q * (T + U)
+HALF = I // 2
+NB = 256
+NA = 512
+
+
+def tile_attend_bridged_two_kernel(tc, query, keys_words, keys_scales, notes_words, notes_scales, lam,
+                                    offs, offs2, offs3, offs4, offs5, out):
+    nc = tc.nc
+    with ExitStack() as ctx:
+        pool = ctx.enter_context(tc.tile_pool(name="held", bufs=1))
+        psum = ctx.enter_context(tc.psum_pool(name="psum", bufs=1))
+
+        q_raw = pool.tile([P, PACK, Q], F32, name="q_raw")
+        q_bf = pool.tile([P, Q, PACK], BF16, name="q_bf", align_bytes=64)
+        q_codes = pool.tile([P, Q], U32, name="q_codes", align_bytes=64)
+        q_plane = pool.tile([P, Q], U8, name="q_plane", align_bytes=64)
+        n_words = pool.tile([P, 2 * U], U8, name="n_words", align_bytes=64)
+        n_plane = pool.tile([P, U], U8, name="n_plane", align_bytes=64)
+        k_words = pool.tile([P, T], I32, name="k_words", align_bytes=64)
+        k_plane = pool.tile([P, T], U8, name="k_plane", align_bytes=64)
+        lam_sb = pool.tile([P, 1], F32, name="lam_sb")
+        l1 = pool.tile([P, I // 16], U16, name="l1")
+        l2 = pool.tile([P, I // 16], U16, name="l2")
+        l3 = pool.tile([P, I // 16], U16, name="l3")
+        l4 = pool.tile([P, I // 16], U16, name="l4")
+        l5 = pool.tile([P, I // 16], U16, name="l5")
+        a_sb = pool.tile([P, T], F32, name="a_sb")
+        b_sb = pool.tile([P, U], F32, name="b_sb")
+        ga = pool.tile([P, I], F32, name="ga")
+        gb = pool.tile([P, I], F32, name="gb")
+        f1 = pool.tile([P, Z], F32, name="f1")
+        f2 = pool.tile([P, Z], F32, name="f2")
+        cc = pool.tile([P, Z], F32, name="cc")
+        gc = pool.tile([P, HALF], F32, name="gc")
+        y0 = pool.tile([P, HALF], F32, name="y0")
+        y1 = pool.tile([P, HALF], F32, name="y1")
+
+        nc.vector.memset(n_plane[:].bitcast(I32), 0)
+        nc.vector.memset(k_plane[:].bitcast(I32), 0)
+
+        nc.sync.dma_start(out=q_raw[:], in_=query.rearrange("(p j) w -> p j w", j=PACK))
+        nc.sync.dma_start(out=n_words[:].bitcast(I32), in_=notes_words[0].bitcast(I32))
+        for g in range(4):
+            nc.scalar.dma_start(out=n_plane[32 * g : 32 * g + 4, :].bitcast(I32),
+                                in_=notes_scales[0, 4 * g : 4 * g + 4, :].bitcast(I32))
+        nc.sync.dma_start(l2[:], offs2)
+        nc.sync.dma_start(out=k_words[:], in_=keys_words[0].rearrange("p n t -> p (n t)").bitcast(I32))
+        for g in range(4):
+            nc.sync.dma_start(out=k_plane[32 * g : 32 * g + 4, :].bitcast(I32),
+                              in_=keys_scales[0, 4 * g : 4 * g + 4, :].bitcast(I32))
+        nc.sync.dma_start(l4[:], offs4)
+        nc.sync.dma_start(l1[:], offs)
+        nc.sync.dma_start(l3[:], offs3)
+        nc.sync.dma_start(l5[:], offs5)
+        nc.gpsimd.dma_start(out=lam_sb[:], in_=lam)
+
+        nc.vector.memset(f2[:], 0.0)
+        nc.vector.memset(f1[:], 0.0)
+
+        nc.vector.tensor_copy(out=q_bf[:], in_=q_raw[:].rearrange("p j w -> p w j"))
+        nc.vector.quantize_mx(out=q_codes[:].bitcast(FP8X4), scales=q_plane[:],
+                              in_=q_bf[:].rearrange("p w j -> p (w j)"))
+
+        for c in range(U // NB):
+            bank = psum.tile([P, NB], F32, name="b_bank%d" % c)
+            nc.tensor.matmul_mx(out=bank[:], lhsT=q_codes[:].bitcast(FP8X4), lhsT_scale=q_plane[:],
+                                rhs=n_words[:, 2 * NB * c : 2 * NB * (c + 1)].bitcast(FP4X4),
+                                rhs_scale=n_plane[:, NB * c : NB * (c + 1)], start=True, stop=True)
+            if c % 2 == 0:
+                nc.scalar.copy(out=b_sb[:, NB * c : NB * (c + 1)], in_=bank[:])
+            else:
+                nc.vector.tensor_copy(out=b_sb[:, NB * c : NB * (c + 1)], in_=bank[:])
+
+        nc.vector.tensor_copy(gb[:, :HALF], b_sb[:].indirect(l2[:, : HALF // 16]))
+        nc.scalar.activation(gb[:, HALF:], b_sb[:].indirect(l2[:, HALF // 16 :]), COPY)
+        nc.vector.tensor_copy(f2[:].indirect(l4[:]), gb[:])
+
+        for c in range(T // NA):
+            bank = psum.tile([P, NA], F32, name="a_bank%d" % c)
+            nc.tensor.matmul_mx(out=bank[:], lhsT=q_codes[:].bitcast(FP8X4), lhsT_scale=q_plane[:],
+                                rhs=k_words[:, NA * c : NA * (c + 1)].bitcast(FP8X4),
+                                rhs_scale=k_plane[:, NA * c : NA * (c + 1)], start=True, stop=True)
+            nc.scalar.copy(out=a_sb[:, NA * c : NA * (c + 1)], in_=bank[:])
+
+        nc.scalar.activation(ga[:], a_sb[:].indirect(l1[:]), COPY)
+        nc.vector.tensor_copy(f1[:].indirect(l3[:]), ga[:])
+
+        nc.vector.scalar_tensor_tensor(out=cc[:], in0=f2[:], scalar=lam_sb[:], in1=f1[:], op0=MULT, op1=ADD)
+
+        nc.vector.tensor_tensor(y0[:], cc[:].indirect(l5[:, : HALF // 16]), ga[:, :HALF], ADD)
+        nc.scalar.activation(gc[:], cc[:].indirect(l5[:, HALF // 16 :]), COPY)
+        nc.sync.dma_start(out=out[:, :HALF], in_=y0[:])
+        nc.vector.tensor_tensor(y1[:], gc[:], ga[:, HALF:], ADD)
+        nc.sync.dma_start(out=out[:, HALF:], in_=y1[:])

@@ -21,6 +21,7 @@ FLOPS = 2 * D * Q * (T + U)
 HALF = I // 2
 NB = 256
 NA = 512
+QV = 72
 
 
 def tile_attend_bridged_two_kernel(tc, query, keys_words, keys_scales, notes_words, notes_scales, lam,
@@ -34,7 +35,7 @@ def tile_attend_bridged_two_kernel(tc, query, keys_words, keys_scales, notes_wor
         q_bf = pool.tile([P, Q, PACK], BF16, name="q_bf", align_bytes=64)
         q_codes = pool.tile([P, Q], U32, name="q_codes", align_bytes=64)
         q_plane = pool.tile([P, Q], U8, name="q_plane", align_bytes=64)
-        n_words = pool.tile([P, 2 * U], U8, name="n_words", align_bytes=64)
+        n_words = [pool.tile([P, U], U8, name="n_words%d" % h, align_bytes=64) for h in range(2)]
         n_plane = pool.tile([P, U], U8, name="n_plane", align_bytes=64)
         k_words = pool.tile([P, T], I32, name="k_words", align_bytes=64)
         k_plane = pool.tile([P, T], U8, name="k_plane", align_bytes=64)
@@ -59,12 +60,13 @@ def tile_attend_bridged_two_kernel(tc, query, keys_words, keys_scales, notes_wor
         nc.vector.memset(k_plane[:].bitcast(I32), 0)
 
         nc.sync.dma_start(out=q_raw[:], in_=query.rearrange("(p j) w -> p j w", j=PACK))
-        nc.sync.dma_start(out=n_words[:].bitcast(I32), in_=notes_words[0].bitcast(I32))
+        nc.sync.dma_start(out=n_words[0][:].bitcast(I32), in_=notes_words[0, :, :U].bitcast(I32))
         for g in range(4):
-            nc.scalar.dma_start(out=n_plane[32 * g : 32 * g + 4, :].bitcast(I32),
+            nc.sync.dma_start(out=n_plane[32 * g : 32 * g + 4, :].bitcast(I32),
                                 in_=notes_scales[0, 4 * g : 4 * g + 4, :].bitcast(I32))
-        nc.sync.dma_start(l2[:], offs2)
+        nc.sync.dma_start(out=n_words[1][:].bitcast(I32), in_=notes_words[0, :, U:].bitcast(I32))
         nc.sync.dma_start(out=k_words[:], in_=keys_words[0].rearrange("p n t -> p (n t)").bitcast(I32))
+        nc.sync.dma_start(l2[:], offs2)
         for g in range(4):
             nc.sync.dma_start(out=k_plane[32 * g : 32 * g + 4, :].bitcast(I32),
                               in_=keys_scales[0, 4 * g : 4 * g + 4, :].bitcast(I32))
@@ -72,31 +74,32 @@ def tile_attend_bridged_two_kernel(tc, query, keys_words, keys_scales, notes_wor
         nc.sync.dma_start(l1[:], offs)
         nc.sync.dma_start(l3[:], offs3)
         nc.sync.dma_start(l5[:], offs5)
-        nc.gpsimd.dma_start(out=lam_sb[:], in_=lam)
+        nc.sync.dma_start(out=lam_sb[:], in_=lam)
 
         nc.vector.memset(f2[:], 0.0)
         nc.vector.memset(f1[:], 0.0)
 
-        nc.vector.tensor_copy(out=q_bf[:], in_=q_raw[:].rearrange("p j w -> p w j"))
+        nc.vector.tensor_copy(out=q_bf[:, : QV, :], in_=q_raw[:, :, : QV].rearrange("p j w -> p w j"))
+        nc.scalar.copy(out=q_bf[:, QV :, :], in_=q_raw[:, :, QV :].rearrange("p j w -> p w j"))
         nc.vector.quantize_mx(out=q_codes[:].bitcast(FP8X4), scales=q_plane[:],
                               in_=q_bf[:].rearrange("p w j -> p (w j)"))
 
-        for c in range(U // NB):
-            bank = psum.tile([P, NB], F32, name="b_bank%d" % c)
+        for c, (u0, u1) in enumerate(((0, 256), (256, 512), (512, 768), (768, 896), (896, 1024))):
+            bank = psum.tile([P, u1 - u0], F32, name="b_bank%d" % c, tag="bank%d" % c)
             nc.tensor.matmul_mx(out=bank[:], lhsT=q_codes[:].bitcast(FP8X4), lhsT_scale=q_plane[:],
-                                rhs=n_words[:, 2 * NB * c : 2 * NB * (c + 1)].bitcast(FP4X4),
-                                rhs_scale=n_plane[:, NB * c : NB * (c + 1)], start=True, stop=True)
-            if c % 2 == 0:
-                nc.scalar.copy(out=b_sb[:, NB * c : NB * (c + 1)], in_=bank[:])
+                                rhs=n_words[u0 // 512][:, 2 * (u0 % 512) : 2 * (u0 % 512 + u1 - u0)].bitcast(FP4X4),
+                                rhs_scale=n_plane[:, u0:u1], start=True, stop=True)
+            if c in (1, 3, 4):
+                nc.scalar.copy(out=b_sb[:, u0:u1], in_=bank[:])
             else:
-                nc.vector.tensor_copy(out=b_sb[:, NB * c : NB * (c + 1)], in_=bank[:])
+                nc.vector.tensor_copy(out=b_sb[:, u0:u1], in_=bank[:])
 
         nc.vector.tensor_copy(gb[:, :HALF], b_sb[:].indirect(l2[:, : HALF // 16]))
         nc.scalar.activation(gb[:, HALF:], b_sb[:].indirect(l2[:, HALF // 16 :]), COPY)
         nc.vector.tensor_copy(f2[:].indirect(l4[:]), gb[:])
 
         for c in range(T // NA):
-            bank = psum.tile([P, NA], F32, name="a_bank%d" % c)
+            bank = psum.tile([P, NA], F32, name="a_bank%d" % c, tag="bank%d" % (4 - c))
             nc.tensor.matmul_mx(out=bank[:], lhsT=q_codes[:].bitcast(FP8X4), lhsT_scale=q_plane[:],
                                 rhs=k_words[:, NA * c : NA * (c + 1)].bitcast(FP8X4),
                                 rhs_scale=k_plane[:, NA * c : NA * (c + 1)], start=True, stop=True)

from contextlib import ExitStack

import concourse.mybir as mybir

F32 = mybir.dt.float32
BF16 = mybir.dt.bfloat16
I32 = mybir.dt.int32
U32 = mybir.dt.uint32
U16 = mybir.dt.uint16
U8 = mybir.dt.uint8
FP8X4 = mybir.dt.float8_e4m3fn_x4
FP4X4 = mybir.dt.float4_e2m1fn_x4
MULT = mybir.AluOpType.mult
ADD = mybir.AluOpType.add
COPY = mybir.ActivationFunctionType.Copy

P = 128
PACK = 4
D, T, U, Z, I, Q = 512, 1024, 1024, 1024, 512, 128
FLOPS = 2 * D * Q * (T + U)
HALF = I // 2
NB = 256
NA = 512
QV = 72


def tile_attend_bridged_two_kernel(tc, query, keys_words, keys_scales, notes_words, notes_scales, lam,
                                    offs, offs2, offs3, offs4, offs5, out):
    nc = tc.nc
    with ExitStack() as ctx:
        pool = ctx.enter_context(tc.tile_pool(name="held", bufs=1))
        psum = ctx.enter_context(tc.psum_pool(name="psum", bufs=1))

        q_raw = pool.tile([P, PACK, Q], F32, name="q_raw")
        q_bf = pool.tile([P, Q, PACK], BF16, name="q_bf", align_bytes=64)
        q_codes = pool.tile([P, Q], U32, name="q_codes", align_bytes=64)
        q_plane = pool.tile([P, Q], U8, name="q_plane", align_bytes=64)
        n_words = [pool.tile([P, U], U8, name="n_words%d" % h, align_bytes=64) for h in range(2)]
        n_plane = pool.tile([P, U], U8, name="n_plane", align_bytes=64)
        k_words = pool.tile([P, T], I32, name="k_words", align_bytes=64)
        k_plane = pool.tile([P, T], U8, name="k_plane", align_bytes=64)
        lam_sb = pool.tile([P, 1], F32, name="lam_sb")
        l1 = pool.tile([P, I // 16], U16, name="l1")
        l2 = pool.tile([P, I // 16], U16, name="l2")
        l3 = pool.tile([P, I // 16], U16, name="l3")
        l4 = pool.tile([P, I // 16], U16, name="l4")
        l5 = pool.tile([P, I // 16], U16, name="l5")
        a_sb = pool.tile([P, T], F32, name="a_sb")
        b_sb = pool.tile([P, U], F32, name="b_sb")
        ga = pool.tile([P, I], F32, name="ga")
        gb = pool.tile([P, I], F32, name="gb")
        f1 = pool.tile([P, Z], F32, name="f1")
        f2 = pool.tile([P, Z], F32, name="f2")
        cc = pool.tile([P, Z], F32, name="cc")
        gc = pool.tile([P, HALF], F32, name="gc")
        y0 = pool.tile([P, HALF], F32, name="y0")
        y1 = pool.tile([P, HALF], F32, name="y1")

        nc.vector.memset(n_plane[:].bitcast(I32), 0)
        nc.vector.memset(k_plane[:].bitcast(I32), 0)

        nc.sync.dma_start(out=q_raw[:], in_=query.rearrange("(p j) w -> p j w", j=PACK))
        nc.sync.dma_start(out=n_words[0][:].bitcast(I32), in_=notes_words[0, :, :U].bitcast(I32))
        for g in range(4):
            nc.sync.dma_start(out=n_plane[32 * g : 32 * g + 4, :].bitcast(I32),
                                in_=notes_scales[0, 4 * g : 4 * g + 4, :].bitcast(I32))
        nc.sync.dma_start(out=n_words[1][:].bitcast(I32), in_=notes_words[0, :, U:].bitcast(I32))
        nc.sync.dma_start(out=k_words[:], in_=keys_words[0].rearrange("p n t -> p (n t)").bitcast(I32))
        nc.sync.dma_start(l2[:], offs2)
        for g in range(4):
            nc.sync.dma_start(out=k_plane[32 * g : 32 * g + 4, :].bitcast(I32),
                              in_=keys_scales[0, 4 * g : 4 * g + 4, :].bitcast(I32))
        nc.sync.dma_start(l4[:], offs4)
        nc.sync.dma_start(l1[:], offs)
        nc.sync.dma_start(l3[:], offs3)
        nc.sync.dma_start(l5[:], offs5)
        nc.sync.dma_start(out=lam_sb[:], in_=lam)

        nc.vector.memset(f2[:], 0.0)
        nc.vector.memset(f1[:], 0.0)

        nc.vector.tensor_copy(out=q_bf[:, : QV, :], in_=q_raw[:, :, : QV].rearrange("p j w -> p w j"))
        nc.scalar.copy(out=q_bf[:, QV :, :], in_=q_raw[:, :, QV :].rearrange("p j w -> p w j"))
        nc.vector.quantize_mx(out=q_codes[:].bitcast(FP8X4), scales=q_plane[:],
                              in_=q_bf[:].rearrange("p w j -> p (w j)"))

        for c, (u0, u1) in enumerate(((0, 256), (256, 512), (512, 768), (768, 896), (896, 1024))):
            bank = psum.tile([P, u1 - u0], F32, name="b_bank%d" % c, tag="bank%d" % c)
            nc.tensor.matmul_mx(out=bank[:], lhsT=q_codes[:].bitcast(FP8X4), lhsT_scale=q_plane[:],
                                rhs=n_words[u0 // 512][:, 2 * (u0 % 512) : 2 * (u0 % 512 + u1 - u0)].bitcast(FP4X4),
                                rhs_scale=n_plane[:, u0:u1], start=True, stop=True)
            if c in (1, 3, 4):
                nc.scalar.copy(out=b_sb[:, u0:u1], in_=bank[:])
            else:
                nc.vector.tensor_copy(out=b_sb[:, u0:u1], in_=bank[:])

        nc.vector.tensor_copy(gb[:, :HALF], b_sb[:].indirect(l2[:, : HALF // 16]))
        nc.scalar.activation(gb[:, HALF:], b_sb[:].indirect(l2[:, HALF // 16 :]), COPY)
        nc.vector.tensor_copy(f2[:].indirect(l4[:]), gb[:])

        for c in range(T // NA):
            bank = psum.tile([P, NA], F32, name="a_bank%d" % c, tag="bank%d" % (4 - c))
            nc.tensor.matmul_mx(out=bank[:], lhsT=q_codes[:].bitcast(FP8X4), lhsT_scale=q_plane[:],
                                rhs=k_words[:, NA * c : NA * (c + 1)].bitcast(FP8X4),
                                rhs_scale=k_plane[:, NA * c : NA * (c + 1)], start=True, stop=True)
            nc.scalar.copy(out=a_sb[:, NA * c : NA * (c + 1)], in_=bank[:])

        nc.scalar.activation(ga[:], a_sb[:].indirect(l1[:]), COPY)
        nc.vector.tensor_copy(f1[:].indirect(l3[:]), ga[:])

        nc.vector.scalar_tensor_tensor(out=cc[:], in0=f2[:], scalar=lam_sb[:], in1=f1[:], op0=MULT, op1=ADD)

        nc.vector.tensor_tensor(y0[:], cc[:].indirect(l5[:, : HALF // 16]), ga[:, :HALF], ADD)
        nc.scalar.activation(gc[:], cc[:].indirect(l5[:, HALF // 16 :]), COPY)
        nc.sync.dma_start(out=out[:, :HALF], in_=y0[:])
        nc.vector.tensor_tensor(y1[:], gc[:], ga[:, HALF:], ADD)
        nc.sync.dma_start(out=out[:, HALF:], in_=y1[:])
